import numpy as np, ml_dtypes
CORES = [2,3,42,43,82,83,122,123]
N = 8
import mx_ref
NC, GR, GC, T = 256, 2, 4, 4
TA, TB = T // GC, T // GR
BF = ml_dtypes.bfloat16
def setup_inputs(rng):
    def f(*shape):
        return mx_ref.flush((rng.standard_normal(shape, dtype=np.float32) * np.exp2(rng.integers(-2, 3, shape[:-1] + (1,)))).astype(BF))
    return {"a": f(N, 128, TA * 512), "b": f(N, 128, TB * 4 * NC)}
def setup_inputs_blocks(rng):
    d = setup_inputs(rng)
    for k in ("a", "b"): d[k] = mx_ref.spread(d[k], rng, 1)
    return d
def setup_inputs_wide(rng):
    d = setup_inputs(rng)
    for k in ("a", "b"): d[k] = mx_ref.flush((d[k].astype(np.float32) * np.exp2(rng.integers(-8, 9, (N, 1, 1))).astype(np.float32)).astype(BF))
    return d
def setup_inputs_zeros(rng):
    d = setup_inputs(rng); v = d["b"].reshape(N, 128, -1, 4).copy()
    v[np.broadcast_to((rng.random((N, 1, v.shape[2], 1)) < 0.33), v.shape)] = 0
    d["b"] = v.reshape(d["b"].shape)
    return d
def reference(a, b):
    A = lambda i, s: mx_ref.quantize(a[i * GC + s // TA][:, 512 * (s % TA):512 * (s % TA) + 512])
    B = lambda s, j: mx_ref.quantize(b[(s // TB) * GC + j][:, 4 * NC * (s % TB):4 * NC * (s % TB) + 4 * NC])
    y = np.zeros((N, 128, NC), np.float32)
    for r in range(N):
        for s in range(T):
            p = mx_ref.matmul(A(r // GC, s), B(s, r % GC))
            y[r] = p if s == 0 else y[r] + p
    return {"y": y}

@@ -1,0 +1,121 @@
+from concourse.mybir import dt
+
+GR, GC = 2, 4
+NC = 256
+NA = 128
+TB = 2
+
+SCRATCH = {
+    "abf": ("sbuf", [128, 4 * NA], "bfloat16"),
+    "bbf": ("sbuf", [128, 4 * NC * TB], "bfloat16"),
+    "qa": ("sbuf", [128, NA * GC], "float8_e4m3fn_x4"),
+    "sa": ("sbuf", [128, NA * GC], "uint8"),
+    "qb": ("sbuf", [128, NC * GR * TB], "float8_e4m3fn_x4"),
+    "sb": ("sbuf", [128, NC * GR * TB], "uint8"),
+    "acc": ("psum", [128, 512], "float32"),
+    "ysb": ("sbuf", [128, NC], "float32"),
+}
+SEMAPHORES = ["lda", "ldb0", "ldb1",
+              "qda", "qdb0", "qdb1",
+              "axc", "axs",
+              "an",
+              "af",
+              "rb0", "rb1",
+              "sent", "mm", "cp", "st"]
+
+
+def _bits(m):
+    return bin(m).count("1")
+
+
+def rank_program(g, core, T, topo):
+    rank = T.rank_of(core)
+    if rank is None:
+        return
+    S = T.sem
+    i, j = divmod(rank, GC)
+    row = [T.cores[i * GC + s] for s in range(GC)]
+    partner = T.cores[(1 - i) * GC + j]
+    here = [s for s in range(GC) if topo.chip(row[s]) == topo.chip(core)]
+    there = [s for s in range(GC) if topo.chip(row[s]) != topo.chip(core)]
+    assert len(here) == 2 and len(there) == 2
+    k = here.index(j)
+    nb = here[1 - k]
+    xs = there[k]
+    fs = there[1 - k]
+    assert topo.may_write(core, row[xs]) and topo.may_write(core, partner)
+
+    m_off = topo.mask(core, row[xs]) & topo.mask(core, partner)
+    m_on = topo.mask(core, row[nb]) & ~m_off
+    n_off, n_on = _bits(m_off), _bits(m_on)
+    sent = [0]
+
+    def put(buf, codes, c0, c1, dst, sem, mask):
+        if codes:
+            o, s = buf[:, c0:c1].bitcast(dt.uint8), buf[:, c0:c1].bitcast(dt.uint8)
+        else:
+            o, s = buf[:, c0:c1], buf[:, c0:c1]
+        rid, pid, _ = topo.addr(dst)
+        g.remote_dma(o, s, sem, S.sent, pid, rid, mask)
+        sent[0] += _bits(mask)
+
+    g.sync.dma_start(T.abf[:], T.a[:]).then_inc(S.lda, 16)
+    g.scalar.dma_start(T.bbf[:, 0:4 * NC], T.b[:, 0:4 * NC]).then_inc(S.ldb0, 16)
+    g.sync.dma_start(T.bbf[:, 4 * NC:8 * NC], T.b[:, 4 * NC:8 * NC]).then_inc(S.ldb1, 16)
+
+    a0 = NA * j
+    b0 = NC * TB * i
+    v = g.vector
+    v.wait_ge(S.lda, 16)
+    v.quantize_mx(T.qa[:, a0:a0 + NA], T.sa[:, a0:a0 + NA], T.abf[:]).then_inc(S.qda, 1)
+    v.wait_ge(S.ldb0, 16)
+    v.quantize_mx(T.qb[:, b0:b0 + NC], T.sb[:, b0:b0 + NC], T.bbf[:, 0:4 * NC]).then_inc(S.qdb0, 1)
+    v.wait_ge(S.ldb1, 16)
+    v.quantize_mx(T.qb[:, b0 + NC:b0 + 2 * NC], T.sb[:, b0 + NC:b0 + 2 * NC], T.bbf[:, 4 * NC:8 * NC]).then_inc(S.qdb1, 1)
+
+    g.wait_ge(S.qda, 1)
+    put(T.qa, True, a0, a0 + NA, row[xs], S.axc, m_off)
+    put(T.sa, False, a0, a0 + NA, row[xs], S.axs, m_off)
+    g.wait_ge(S.qdb0, 1)
+    put(T.qb, True, b0, b0 + NC, partner, S.rb0, m_off)
+    g.wait_ge(S.qdb1, 1)
+    put(T.sb, False, b0, b0 + 2 * NC, partner, S.rb0, m_off)
+    put(T.qb, True, b0 + NC, b0 + 2 * NC, partner, S.rb1, m_off)
+    put(T.qa, True, a0, a0 + NA, row[nb], S.an, m_on)
+    put(T.sa, False, a0, a0 + NA, row[nb], S.an, m_on)
+    x0 = NA * xs
+    g.wait_ge(S.axc, n_off)
+    put(T.qa, True, x0, x0 + NA, row[nb], S.af, m_on)
+    g.wait_ge(S.axs, n_off)
+    put(T.sa, False, x0, x0 + NA, row[nb], S.af, m_on)
+
+    a_need = {j: (0.0, [("qda", 1)]),
+              nb: (1.0, [("an", 2 * n_on)]),
+              xs: (2.0, [("axc", n_off), ("axs", n_off)]),
+              fs: (3.0, [("af", 2 * n_on)])}
+    b_need = {}
+    for m in range(TB):
+        b_need[TB * i + m] = (0.0, [("qdb%d" % m, 1)])
+    b_need[TB * (1 - i)] = (2.5, [("rb0", 2 * n_off)])
+    b_need[TB * (1 - i) + 1] = (4.0, [("rb0", 2 * n_off), ("rb1", n_off)])
+    order = sorted(range(GC), key=lambda s: max(a_need[s][0], b_need[s][0]))
+    t = g.tensor
+    seen = []
+    mmi = None
+    for n, s in enumerate(order):
+        for name, val in a_need[s][1] + b_need[s][1]:
+            if name not in seen:
+                seen.append(name)
+                t.wait_ge(S[name], val)
+        mmi = t.matmul_mx(T.acc[:, 0:NC],
+                          T.qa[:, NA * s:NA * s + NA], T.sa[:, NA * s:NA * s + NA],
+                          T.qb[:, NC * s:NC * s + NC], T.sb[:, NC * s:NC * s + NC],
+                          n == 0, n == GC - 1)
+    mmi.then_inc(S.mm, 1)
+
+    v.wait_ge(S.mm, 1)
+    v.tensor_copy(T.ysb[:], T.acc[:, 0:NC]).then_inc(S.cp, 1)
+    g.sync.wait_ge(S.cp, 1)
+    g.sync.dma_start(T.y[:], T.ysb[:]).then_inc(S.st, 16)
+    g.sync.wait_ge(S.st, 16)
+    g.wait_ge(S.sent, sent[0])

@@ -1,9 +1,12 @@
 from concourse.mybir import dt
+from concourse.bass import DstId, RemoteDMATransfer
 
 GR, GC = 2, 4
 NC = 256
 NA = 128
 TB = 2
+NSIM = 128
+NH = 2
 
 SCRATCH = {
     "abf": ("sbuf", [128, 4 * NA], "bfloat16"),
@@ -20,6 +23,7 @@ SEMAPHORES = ["lda", "ldb0", "ldb1",
               "axc", "axs",
               "an",
               "af",
+              "hs", "hc",
               "rb0", "rb1",
               "sent", "mm", "cp", "st"]
 
@@ -28,14 +32,64 @@ def _bits(m):
     return bin(m).count("1")
 
 
+def _split(m, n):
+    e = [1 << b for b in range(m.bit_length()) if (m >> b) & 1]
+    w = len(e) // n
+    return [sum(e[q * w:(q + 1) * w]) for q in range(n)]
+
+
+def _partner(T, rank):
+    i, j = divmod(rank, GC)
+    return T.cores[(1 - i) * GC + j]
+
+
+def _relays(T, topo, rcore):
+    mine = [c for c in range(NSIM) if topo.chip(c) == topo.chip(rcore)]
+    ranks = [c for c in mine if T.rank_of(c) is not None]
+    free = [c for c in mine if T.rank_of(c) is None and topo.die(c) != topo.die(rcore)
+            and all(topo.may_write(c, _partner(T, T.rank_of(r))) for r in ranks)]
+    k = ranks.index(rcore)
+    got = free[NH * k:NH * k + NH]
+    assert len(got) == NH
+    return got
+
+
+def _u8(buf, codes, c0, c1):
+    return buf[:, c0:c1].bitcast(dt.uint8) if codes else buf[:, c0:c1]
+
+
+def _relay_program(g, core, T, topo):
+    S = T.sem
+    for rcore in T.cores:
+        if topo.chip(rcore) != topo.chip(core):
+            continue
+        hs = _relays(T, topo, rcore)
+        if core not in hs:
+            continue
+        h = hs.index(core)
+        rank = T.rank_of(rcore)
+        partner = _partner(T, rank)
+        n_in = _bits(_split(topo.mask(rcore, core) & ~topo.mask(rcore, partner), NH)[h])
+        m = topo.mask(core, partner)
+        rid, pid, _ = topo.addr(partner)
+        w = NC // NH
+        c0 = NC * TB * (rank // GC) + w * h
+        g.wait_ge(S.hs, n_in)
+        g.remote_dma(_u8(T.sb, False, c0, c0 + w), _u8(T.sb, False, c0, c0 + w), S.rb0, S.sent, pid, rid, m)
+        g.wait_ge(S.hc, n_in)
+        g.remote_dma(_u8(T.qb, True, c0, c0 + w), _u8(T.qb, True, c0, c0 + w), S.rb0, S.sent, pid, rid, m)
+        g.wait_ge(S.sent, 2 * _bits(m))
+
+
 def rank_program(g, core, T, topo):
     rank = T.rank_of(core)
     if rank is None:
+        _relay_program(g, core, T, topo)
         return
     S = T.sem
     i, j = divmod(rank, GC)
     row = [T.cores[i * GC + s] for s in range(GC)]
-    partner = T.cores[(1 - i) * GC + j]
+    partner = _partner(T, rank)
     here = [s for s in range(GC) if topo.chip(row[s]) == topo.chip(core)]
     there = [s for s in range(GC) if topo.chip(row[s]) != topo.chip(core)]
     assert len(here) == 2 and len(there) == 2
@@ -44,20 +98,29 @@ def rank_program(g, core, T, topo):
     xs = there[k]
     fs = there[1 - k]
     assert topo.may_write(core, row[xs]) and topo.may_write(core, partner)
+    relays = _relays(T, topo, core)
 
     m_off = topo.mask(core, row[xs]) & topo.mask(core, partner)
     m_on = topo.mask(core, row[nb]) & ~m_off
     n_off, n_on = _bits(m_off), _bits(m_on)
+    m_rel = _split(m_on, NH)
     sent = [0]
 
     def put(buf, codes, c0, c1, dst, sem, mask):
-        if codes:
-            o, s = buf[:, c0:c1].bitcast(dt.uint8), buf[:, c0:c1].bitcast(dt.uint8)
-        else:
-            o, s = buf[:, c0:c1], buf[:, c0:c1]
         rid, pid, _ = topo.addr(dst)
-        g.remote_dma(o, s, sem, S.sent, pid, rid, mask)
+        g.remote_dma(_u8(buf, codes, c0, c1), _u8(buf, codes, c0, c1), sem, S.sent, pid, rid, mask)
         sent[0] += _bits(mask)
+
+    def to_relays(buf, codes, c0, sem):
+        w = NC // NH
+        tr = []
+        for h in range(NH):
+            rid, pid, _ = topo.addr(relays[h])
+            ap = _u8(buf, codes, c0 + w * h, c0 + w * h + w)
+            tr.append(RemoteDMATransfer(dst_ids=[DstId(rid=rid, pnc=pid)], dma_engine_mask=m_rel[h],
+                                        remote_sem=sem, src=ap, dst=ap))
+            sent[0] += _bits(m_rel[h])
+        g.remote_dma_fused(tr, local_sem=S.sent)
 
     g.sync.dma_start(T.abf[:], T.a[:]).then_inc(S.lda, 16)
     g.scalar.dma_start(T.bbf[:, 0:4 * NC], T.b[:, 0:4 * NC]).then_inc(S.ldb0, 16)
@@ -77,9 +140,10 @@ def rank_program(g, core, T, topo):
     put(T.qa, True, a0, a0 + NA, row[xs], S.axc, m_off)
     put(T.sa, False, a0, a0 + NA, row[xs], S.axs, m_off)
     g.wait_ge(S.qdb0, 1)
-    put(T.qb, True, b0, b0 + NC, partner, S.rb0, m_off)
+    to_relays(T.sb, False, b0, S.hs)
+    to_relays(T.qb, True, b0, S.hc)
     g.wait_ge(S.qdb1, 1)
-    put(T.sb, False, b0, b0 + 2 * NC, partner, S.rb0, m_off)
+    put(T.sb, False, b0 + NC, b0 + 2 * NC, partner, S.rb1, m_off)
     put(T.qb, True, b0 + NC, b0 + 2 * NC, partner, S.rb1, m_off)
     put(T.qa, True, a0, a0 + NA, row[nb], S.an, m_on)
     put(T.sa, False, a0, a0 + NA, row[nb], S.an, m_on)
@@ -89,6 +153,7 @@ def rank_program(g, core, T, topo):
     g.wait_ge(S.axs, n_off)
     put(T.sa, False, x0, x0 + NA, row[nb], S.af, m_on)
 
+    n_rel = sum(2 * _bits(topo.mask(h, core)) for h in _relays(T, topo, partner))
     a_need = {j: (0.0, [("qda", 1)]),
               nb: (1.0, [("an", 2 * n_on)]),
               xs: (2.0, [("axc", n_off), ("axs", n_off)]),
@@ -96,8 +161,8 @@ def rank_program(g, core, T, topo):
     b_need = {}
     for m in range(TB):
         b_need[TB * i + m] = (0.0, [("qdb%d" % m, 1)])
-    b_need[TB * (1 - i)] = (2.5, [("rb0", 2 * n_off)])
-    b_need[TB * (1 - i) + 1] = (4.0, [("rb0", 2 * n_off), ("rb1", n_off)])
+    b_need[TB * (1 - i)] = (4.0, [("rb0", n_rel)])
+    b_need[TB * (1 - i) + 1] = (3.5, [("rb1", 2 * n_off)])
     order = sorted(range(GC), key=lambda s: max(a_need[s][0], b_need[s][0]))
     t = g.tensor
     seen = []

from concourse.mybir import dt
from concourse.bass import DstId, RemoteDMATransfer

GR, GC = 2, 4
NC = 256
NA = 128
TB = 2
NSIM = 128
NH = 2

SCRATCH = {
    "abf": ("sbuf", [128, 4 * NA], "bfloat16"),
    "bbf": ("sbuf", [128, 4 * NC * TB], "bfloat16"),
    "qa": ("sbuf", [128, NA * GC], "float8_e4m3fn_x4"),
    "sa": ("sbuf", [128, NA * GC], "uint8"),
    "qb": ("sbuf", [128, NC * GR * TB], "float8_e4m3fn_x4"),
    "sb": ("sbuf", [128, NC * GR * TB], "uint8"),
    "acc": ("psum", [128, 512], "float32"),
    "ysb": ("sbuf", [128, NC], "float32"),
}
SEMAPHORES = ["lda", "ldb0", "ldb1",
              "qda", "qdb0", "qdb1",
              "axc", "axs",
              "an",
              "af",
              "hs", "hc",
              "rb0", "rb1",
              "sent", "mm", "cp", "st"]


def _bits(m):
    return bin(m).count("1")


def _split(m, n):
    e = [1 << b for b in range(m.bit_length()) if (m >> b) & 1]
    w = len(e) // n
    return [sum(e[q * w:(q + 1) * w]) for q in range(n)]


def _partner(T, rank):
    i, j = divmod(rank, GC)
    return T.cores[(1 - i) * GC + j]


def _relays(T, topo, rcore):
    mine = [c for c in range(NSIM) if topo.chip(c) == topo.chip(rcore)]
    ranks = [c for c in mine if T.rank_of(c) is not None]
    free = [c for c in mine if T.rank_of(c) is None and topo.die(c) != topo.die(rcore)
            and all(topo.may_write(c, _partner(T, T.rank_of(r))) for r in ranks)]
    k = ranks.index(rcore)
    got = free[NH * k:NH * k + NH]
    assert len(got) == NH
    return got


def _u8(buf, codes, c0, c1):
    return buf[:, c0:c1].bitcast(dt.uint8) if codes else buf[:, c0:c1]


def _relay_program(g, core, T, topo):
    S = T.sem
    for rcore in T.cores:
        if topo.chip(rcore) != topo.chip(core):
            continue
        hs = _relays(T, topo, rcore)
        if core not in hs:
            continue
        h = hs.index(core)
        rank = T.rank_of(rcore)
        partner = _partner(T, rank)
        n_in = _bits(_split(topo.mask(rcore, core) & ~topo.mask(rcore, partner), NH)[h])
        m = topo.mask(core, partner)
        rid, pid, _ = topo.addr(partner)
        w = NC // NH
        c0 = NC * TB * (rank // GC) + w * h
        g.wait_ge(S.hs, n_in)
        g.remote_dma(_u8(T.sb, False, c0, c0 + w), _u8(T.sb, False, c0, c0 + w), S.rb0, S.sent, pid, rid, m)
        g.wait_ge(S.hc, n_in)
        g.remote_dma(_u8(T.qb, True, c0, c0 + w), _u8(T.qb, True, c0, c0 + w), S.rb0, S.sent, pid, rid, m)
        g.wait_ge(S.sent, 2 * _bits(m))


def rank_program(g, core, T, topo):
    rank = T.rank_of(core)
    if rank is None:
        _relay_program(g, core, T, topo)
        return
    S = T.sem
    i, j = divmod(rank, GC)
    row = [T.cores[i * GC + s] for s in range(GC)]
    partner = _partner(T, rank)
    here = [s for s in range(GC) if topo.chip(row[s]) == topo.chip(core)]
    there = [s for s in range(GC) if topo.chip(row[s]) != topo.chip(core)]
    assert len(here) == 2 and len(there) == 2
    k = here.index(j)
    nb = here[1 - k]
    xs = there[k]
    fs = there[1 - k]
    assert topo.may_write(core, row[xs]) and topo.may_write(core, partner)
    relays = _relays(T, topo, core)

    m_off = topo.mask(core, row[xs]) & topo.mask(core, partner)
    m_on = topo.mask(core, row[nb]) & ~m_off
    n_off, n_on = _bits(m_off), _bits(m_on)
    m_rel = _split(m_on, NH)
    sent = [0]

    def put(buf, codes, c0, c1, dst, sem, mask):
        rid, pid, _ = topo.addr(dst)
        g.remote_dma(_u8(buf, codes, c0, c1), _u8(buf, codes, c0, c1), sem, S.sent, pid, rid, mask)
        sent[0] += _bits(mask)

    def to_relays(buf, codes, c0, sem):
        w = NC // NH
        tr = []
        for h in range(NH):
            rid, pid, _ = topo.addr(relays[h])
            ap = _u8(buf, codes, c0 + w * h, c0 + w * h + w)
            tr.append(RemoteDMATransfer(dst_ids=[DstId(rid=rid, pnc=pid)], dma_engine_mask=m_rel[h],
                                        remote_sem=sem, src=ap, dst=ap))
            sent[0] += _bits(m_rel[h])
        g.remote_dma_fused(tr, local_sem=S.sent)

    g.sync.dma_start(T.abf[:], T.a[:]).then_inc(S.lda, 16)
    g.scalar.dma_start(T.bbf[:, 0:4 * NC], T.b[:, 0:4 * NC]).then_inc(S.ldb0, 16)
    g.sync.dma_start(T.bbf[:, 4 * NC:8 * NC], T.b[:, 4 * NC:8 * NC]).then_inc(S.ldb1, 16)

    a0 = NA * j
    b0 = NC * TB * i
    v = g.vector
    v.wait_ge(S.lda, 16)
    v.quantize_mx(T.qa[:, a0:a0 + NA], T.sa[:, a0:a0 + NA], T.abf[:]).then_inc(S.qda, 1)
    v.wait_ge(S.ldb0, 16)
    v.quantize_mx(T.qb[:, b0:b0 + NC], T.sb[:, b0:b0 + NC], T.bbf[:, 0:4 * NC]).then_inc(S.qdb0, 1)
    v.wait_ge(S.ldb1, 16)
    v.quantize_mx(T.qb[:, b0 + NC:b0 + 2 * NC], T.sb[:, b0 + NC:b0 + 2 * NC], T.bbf[:, 4 * NC:8 * NC]).then_inc(S.qdb1, 1)

    g.wait_ge(S.qda, 1)
    put(T.qa, True, a0, a0 + NA, row[xs], S.axc, m_off)
    put(T.sa, False, a0, a0 + NA, row[xs], S.axs, m_off)
    g.wait_ge(S.qdb0, 1)
    to_relays(T.sb, False, b0, S.hs)
    to_relays(T.qb, True, b0, S.hc)
    g.wait_ge(S.qdb1, 1)
    put(T.sb, False, b0 + NC, b0 + 2 * NC, partner, S.rb1, m_off)
    put(T.qb, True, b0 + NC, b0 + 2 * NC, partner, S.rb1, m_off)
    put(T.qa, True, a0, a0 + NA, row[nb], S.an, m_on)
    put(T.sa, False, a0, a0 + NA, row[nb], S.an, m_on)
    x0 = NA * xs
    g.wait_ge(S.axc, n_off)
    put(T.qa, True, x0, x0 + NA, row[nb], S.af, m_on)
    g.wait_ge(S.axs, n_off)
    put(T.sa, False, x0, x0 + NA, row[nb], S.af, m_on)

    n_rel = sum(2 * _bits(topo.mask(h, core)) for h in _relays(T, topo, partner))
    a_need = {j: (0.0, [("qda", 1)]),
              nb: (1.0, [("an", 2 * n_on)]),
              xs: (2.0, [("axc", n_off), ("axs", n_off)]),
              fs: (3.0, [("af", 2 * n_on)])}
    b_need = {}
    for m in range(TB):
        b_need[TB * i + m] = (0.0, [("qdb%d" % m, 1)])
    b_need[TB * (1 - i)] = (4.0, [("rb0", n_rel)])
    b_need[TB * (1 - i) + 1] = (3.5, [("rb1", 2 * n_off)])
    order = sorted(range(GC), key=lambda s: max(a_need[s][0], b_need[s][0]))
    t = g.tensor
    seen = []
    mmi = None
    for n, s in enumerate(order):
        for name, val in a_need[s][1] + b_need[s][1]:
            if name not in seen:
                seen.append(name)
                t.wait_ge(S[name], val)
        mmi = t.matmul_mx(T.acc[:, 0:NC],
                          T.qa[:, NA * s:NA * s + NA], T.sa[:, NA * s:NA * s + NA],
                          T.qb[:, NC * s:NC * s + NC], T.sb[:, NC * s:NC * s + NC],
                          n == 0, n == GC - 1)
    mmi.then_inc(S.mm, 1)

    v.wait_ge(S.mm, 1)
    v.tensor_copy(T.ysb[:], T.acc[:, 0:NC]).then_inc(S.cp, 1)
    g.sync.wait_ge(S.cp, 1)
    g.sync.dma_start(T.y[:], T.ysb[:]).then_inc(S.st, 16)
    g.sync.wait_ge(S.st, 16)
    g.wait_ge(S.sent, sent[0])
